import numpy as np
import ml_dtypes


def mxq(x, axis, fmt="e4m3"):
    dtype, down = {"e4m3": (ml_dtypes.float8_e4m3fn, 7), "e5m2": (ml_dtypes.float8_e5m2, 14)}[fmt]
    v = np.moveaxis(np.asarray(x, np.float32).astype(ml_dtypes.bfloat16).astype(np.float64), axis, -1)
    blocks = v.reshape(v.shape[:-1] + (-1, 32))
    amax = np.abs(blocks).max(-1, keepdims=True)
    byte = np.maximum(np.where(amax > 0, np.frexp(amax)[1] - 1 + 127, 0) - down, 1)
    scale = np.exp2(byte - 127.0)
    codes = (blocks / scale).astype(np.float32).astype(dtype).astype(np.float64)
    return np.moveaxis((codes * scale).reshape(v.shape), -1, axis)


WIDE = False


def mx_kscale(k):
    if not WIDE:
        return np.ones(k)
    levels = np.array([10, -10, 5, -5, 0])
    if k % 512:
        return np.exp2(np.random.permutation(np.resize(levels, k // 32))).repeat(32)
    a = np.empty((k // 512, 16))
    for p in range(k // 512):
        a[p, :8] = np.random.permutation(np.resize(levels, 8))
        for g in range(8):
            far = levels[np.abs(levels - a[p, g]) >= 10]
            a[p, g + 8] = far[np.random.randint(len(far))]
    return np.exp2(a.ravel()).repeat(32)


def f64(x):
    return np.asarray(x).astype(np.float64)


def striped(idx):
    return np.tile(idx.reshape(-1, 16).T, (8, 1)).astype(np.uint16)


def unstriped(offs):
    return offs[:16].T.reshape(-1).astype(np.int64)


def pack_weight(w):
    k, n = w.shape
    w = f64(np.asarray(w, np.float32).astype(ml_dtypes.bfloat16)).reshape(k // 32, 32, n)
    amax = np.abs(w).max(1)
    byte = np.clip(np.where(amax > 0, np.frexp(amax)[1] - 1 + 127 - 7, 1), 1, 254)
    scaled = (w * np.exp2(127.0 - byte)[:, None, :]).reshape(k, n).astype(np.float32)
    words = np.ascontiguousarray(scaled.reshape(k // 512, 128, 4, n).transpose(0, 1, 3, 2)).astype(ml_dtypes.float8_e4m3fn).view(np.uint8)
    return words, np.ascontiguousarray(byte.astype(np.uint8).reshape(k // 512, 16, n))


def unpack_weight(words, scales):
    g, p, n, _ = words.shape
    vals = np.ascontiguousarray(words).view(ml_dtypes.float8_e4m3fn).astype(np.float64) * np.repeat(np.exp2(scales.astype(np.float64) - 127.0), 8, axis=1)[..., None]
    return vals.transpose(0, 1, 3, 2).reshape(g * 512, n)


K, T, S, N, U = 1024, 2048, 512, 256, 1024


def setup_inputs():
    n = np.random.standard_normal
    s = mx_kscale(K)[:, None]
    packed_w1 = pack_weight(n((K, N)) / np.sqrt(K) / s)
    return {
        "xT": (n((K, T)) * s).astype(np.float32),
        "w1_words": packed_w1[0],
        "w1_scales": packed_w1[1],
        "gamma": np.random.uniform(0.5, 1.5, (N, U)).astype(np.float32),
        "beta": (0.5 * n((N, U))).astype(np.float32),
        "offs": striped(np.random.permutation(T)[:S]),
        "cls": striped(np.random.randint(0, U, S)),
    }


def reference(xT, w1_words, w1_scales, gamma, beta, offs, cls):
    xq = mxq(f64(xT)[:, unstriped(offs)], 0, "e4m3")
    y = unpack_weight(w1_words, w1_scales).T @ xq
    g = f64(gamma)[:, unstriped(cls)]
    s = f64(beta)[:, unstriped(cls)]
    return y * g + s

@@ -1,0 +1,121 @@
+from contextlib import ExitStack
+
+import concourse.mybir as mybir
+
+F32 = mybir.dt.float32
+BF16 = mybir.dt.bfloat16
+I32 = mybir.dt.int32
+U32 = mybir.dt.uint32
+U16 = mybir.dt.uint16
+U8 = mybir.dt.uint8
+FP8X4 = mybir.dt.float8_e4m3fn_x4
+MULT = mybir.AluOpType.mult
+ADD = mybir.AluOpType.add
+
+K, T, S, N, U = 1024, 2048, 512, 256, 1024
+P = 128
+PACK = 4
+PASSES = K // (P * PACK)
+BLOCKS = N // P
+HALF = S // 2
+FLOPS = 2 * K * N * S
+
+
+def tile_picked_cbn_none_e_kernel(tc, xT, w1_words, w1_scales, gamma, beta, offs, cls, out):
+    nc = tc.nc
+    with ExitStack() as ctx:
+        keep = ctx.enter_context(tc.tile_pool(name="keep", bufs=1))
+        psum = ctx.enter_context(tc.psum_pool(name="psum", bufs=1))
+
+        offs_t = keep.tile([P, S // 16], U16, name="offs_t")
+        cls_t = keep.tile([P, S // 16], U16, name="cls_t")
+        planes = [[keep.tile([P, T], F32, name=f"plane{z}{j}") for j in range(PACK)] for z in range(PASSES)]
+        gam = [keep.tile([P, U], F32, name=f"gam{b}", tag=f"gam{b}") for b in range(BLOCKS)]
+        bet = [keep.tile([P, U], F32, name=f"bet{b}") for b in range(BLOCKS)]
+        w_words = [keep.tile([P, N], U32, name=f"w_words{z}", align_bytes=64) for z in range(PASSES)]
+        w_scales = keep.tile([P, PASSES, N], U8, name="w_scales", align_bytes=64)
+        picked = [keep.tile([P, S, PACK], BF16, name=f"picked{z}", align_bytes=64) for z in range(PASSES)]
+        codes = [keep.tile([P, S], U32, name=f"codes{z}", align_bytes=64) for z in range(PASSES)]
+        scales = [keep.tile([P, S], U8, name=f"scales{z}", align_bytes=64) for z in range(PASSES)]
+        g = [keep.tile([P, S], F32, name=f"g{b}") for b in range(BLOCKS)]
+        s = [keep.tile([P, S], F32, name=f"s{b}") for b in range(BLOCKS)]
+        result = [keep.tile([P, S], F32, name=f"result{b}") for b in range(BLOCKS)]
+        acc = [psum.tile([P, S], F32, name=f"acc{b}") for b in range(BLOCKS)]
+
+        x_rows = xT.rearrange("(z p j) t -> z j p t", z=PASSES, j=PACK)
+        scale_rows = w1_scales.rearrange("z (q r) c -> r q z c", r=4)
+
+        def load_plane(z, j):
+            nc.sync.dma_start(out=planes[z][j][:], in_=x_rows[z, j])
+
+        def load_table(tile, table, b):
+            nc.sync.dma_start(out=tile[:], in_=table[b * P : (b + 1) * P, :])
+
+        def load_weights(z):
+            nc.sync.dma_start(out=w_words[z][:].bitcast(I32), in_=w1_words[z].rearrange("p c r -> p (c r)").bitcast(I32))
+
+        def pick(z, j, lo, hi):
+            nc.vector.tensor_copy(picked[z][:, lo:hi, j], planes[z][j][:].indirect(offs_t[:, lo // 16 : hi // 16]))
+
+        def quantise(z, lo, hi):
+            nc.vector.quantize_mx(
+                out=codes[z][:, lo:hi].bitcast(FP8X4),
+                scales=scales[z][:, lo:hi],
+                in_=picked[z][:, lo:hi, :].rearrange("p s j -> p (s j)"),
+            )
+
+        def look_up(dst, tile):
+            nc.vector.tensor_copy(dst[:], tile[:].indirect(cls_t[:]))
+
+        def multiply(z):
+            for b in range(BLOCKS):
+                cols = slice(b * P, (b + 1) * P)
+                nc.tensor.matmul_mx(
+                    out=acc[b][:],
+                    lhsT=w_words[z][:, cols].bitcast(FP8X4),
+                    lhsT_scale=w_scales[:, z, cols],
+                    rhs=codes[z][:].bitcast(FP8X4),
+                    rhs_scale=scales[z][:],
+                    start=(z == 0),
+                    stop=(z == PASSES - 1),
+                )
+
+        nc.vector.memset(w_scales[:].bitcast(I32), 0)
+        load_plane(0, 0)
+        nc.sync.dma_start(offs_t[:], offs)
+        load_plane(0, 1)
+        nc.sync.dma_start(cls_t[:], cls)
+        for r in range(4):
+            nc.scalar.dma_start(out=w_scales[r:P:32, :, :].bitcast(I32), in_=scale_rows[r].bitcast(I32))
+        load_plane(0, 2)
+        load_plane(0, 3)
+        load_weights(0)
+        load_table(gam[1], gamma, 1)
+        load_table(bet[0], beta, 0)
+        load_table(bet[1], beta, 1)
+        for j in range(PACK):
+            load_plane(1, j)
+        load_weights(1)
+        load_table(gam[0], gamma, 0)
+
+        for j in range(PACK):
+            pick(0, j, 0, S)
+        look_up(g[1], gam[1])
+        quantise(0, 0, S)
+        multiply(0)
+        look_up(s[0], bet[0])
+        look_up(s[1], bet[1])
+        for j in range(PACK - 1):
+            pick(1, j, 0, S)
+        pick(1, PACK - 1, 0, HALF)
+        pick(1, PACK - 1, HALF, S)
+        quantise(1, 0, HALF)
+        quantise(1, HALF, S)
+        multiply(1)
+        look_up(g[0], gam[0])
+        scaled = [keep.tile([P, S], F32, name="scaled0"), keep.tile([P, S], F32, name="scaled1", tag="gam0")]
+        for b in range(BLOCKS):
+            nc.vector.tensor_tensor(scaled[b][:], acc[b][:], g[b][:], MULT)
+        for b in range(BLOCKS):
+            nc.vector.tensor_tensor(result[b][:], scaled[b][:], s[b][:], ADD)
+            nc.sync.dma_start(out=out[b * P : (b + 1) * P, :], in_=result[b][:])

@@ -38,7 +38,6 @@ def tile_picked_cbn_none_e_kernel(tc, xT, w1_words, w1_scales, gamma, beta, offs
         codes = [keep.tile([P, S], U32, name=f"codes{z}", align_bytes=64) for z in range(PASSES)]
         scales = [keep.tile([P, S], U8, name=f"scales{z}", align_bytes=64) for z in range(PASSES)]
         g = [keep.tile([P, S], F32, name=f"g{b}") for b in range(BLOCKS)]
-        s = [keep.tile([P, S], F32, name=f"s{b}") for b in range(BLOCKS)]
         result = [keep.tile([P, S], F32, name=f"result{b}") for b in range(BLOCKS)]
         acc = [psum.tile([P, S], F32, name=f"acc{b}") for b in range(BLOCKS)]
 
@@ -80,31 +79,29 @@ def tile_picked_cbn_none_e_kernel(tc, xT, w1_words, w1_scales, gamma, beta, offs
                     stop=(z == PASSES - 1),
                 )
 
-        nc.vector.memset(w_scales[:].bitcast(I32), 0)
+        nc.gpsimd.memset(w_scales[:].bitcast(I32), 0)
         load_plane(0, 0)
         nc.sync.dma_start(offs_t[:], offs)
         load_plane(0, 1)
         nc.sync.dma_start(cls_t[:], cls)
         for r in range(4):
-            nc.scalar.dma_start(out=w_scales[r:P:32, :, :].bitcast(I32), in_=scale_rows[r].bitcast(I32))
+            nc.gpsimd.dma_start(out=w_scales[r:P:32, :, :].bitcast(I32), in_=scale_rows[r].bitcast(I32))
         load_plane(0, 2)
         load_plane(0, 3)
         load_weights(0)
         load_table(gam[1], gamma, 1)
-        load_table(bet[0], beta, 0)
-        load_table(bet[1], beta, 1)
         for j in range(PACK):
             load_plane(1, j)
         load_weights(1)
         load_table(gam[0], gamma, 0)
+        load_table(bet[0], beta, 0)
+        load_table(bet[1], beta, 1)
 
         for j in range(PACK):
             pick(0, j, 0, S)
         look_up(g[1], gam[1])
         quantise(0, 0, S)
         multiply(0)
-        look_up(s[0], bet[0])
-        look_up(s[1], bet[1])
         for j in range(PACK - 1):
             pick(1, j, 0, S)
         pick(1, PACK - 1, 0, HALF)
@@ -116,6 +113,7 @@ def tile_picked_cbn_none_e_kernel(tc, xT, w1_words, w1_scales, gamma, beta, offs
         scaled = [keep.tile([P, S], F32, name="scaled0"), keep.tile([P, S], F32, name="scaled1", tag="gam0")]
         for b in range(BLOCKS):
             nc.vector.tensor_tensor(scaled[b][:], acc[b][:], g[b][:], MULT)
-        for b in range(BLOCKS):
-            nc.vector.tensor_tensor(result[b][:], scaled[b][:], s[b][:], ADD)
-            nc.sync.dma_start(out=out[b * P : (b + 1) * P, :], in_=result[b][:])
+        for b, lo, hi, queue in ((0, 0, S, nc.sync), (1, 0, HALF, nc.scalar), (1, HALF, S, nc.sync)):
+            shift = bet[b][:].indirect(cls_t[:, lo // 16 : hi // 16])
+            nc.vector.tensor_tensor(result[b][:, lo:hi], shift, scaled[b][:, lo:hi], ADD)
+            queue.dma_start(out=out[b * P : (b + 1) * P, lo:hi], in_=result[b][:, lo:hi])

@@ -30,15 +30,15 @@ def tile_picked_cbn_none_e_kernel(tc, xT, w1_words, w1_scales, gamma, beta, offs
         offs_t = keep.tile([P, S // 16], U16, name="offs_t")
         cls_t = keep.tile([P, S // 16], U16, name="cls_t")
         planes = [[keep.tile([P, T], F32, name=f"plane{z}{j}") for j in range(PACK)] for z in range(PASSES)]
-        gam = [keep.tile([P, U], F32, name=f"gam{b}", tag=f"gam{b}") for b in range(BLOCKS)]
+        gam = [keep.tile([P, U], F32, name=f"gam{b}") for b in range(BLOCKS)]
         bet = [keep.tile([P, U], F32, name=f"bet{b}") for b in range(BLOCKS)]
         w_words = [keep.tile([P, N], U32, name=f"w_words{z}", align_bytes=64) for z in range(PASSES)]
         w_scales = keep.tile([P, PASSES, N], U8, name="w_scales", align_bytes=64)
         picked = [keep.tile([P, S, PACK], BF16, name=f"picked{z}", align_bytes=64) for z in range(PASSES)]
-        codes = [keep.tile([P, S], U32, name=f"codes{z}", align_bytes=64) for z in range(PASSES)]
+        codes = [keep.tile([P, S], U32, name=f"codes{z}", tag=f"codes{z}", align_bytes=64) for z in range(PASSES)]
         scales = [keep.tile([P, S], U8, name=f"scales{z}", align_bytes=64) for z in range(PASSES)]
         g = [keep.tile([P, S], F32, name=f"g{b}") for b in range(BLOCKS)]
-        result = [keep.tile([P, S], F32, name=f"result{b}") for b in range(BLOCKS)]
+        scaled = [keep.tile([P, S], F32, name=f"scaled{b}") for b in range(BLOCKS)]
         acc = [psum.tile([P, S], F32, name=f"acc{b}") for b in range(BLOCKS)]
 
         x_rows = xT.rearrange("(z p j) t -> z j p t", z=PASSES, j=PACK)
@@ -88,18 +88,18 @@ def tile_picked_cbn_none_e_kernel(tc, xT, w1_words, w1_scales, gamma, beta, offs
             nc.gpsimd.dma_start(out=w_scales[r:P:32, :, :].bitcast(I32), in_=scale_rows[r].bitcast(I32))
         load_plane(0, 2)
         load_plane(0, 3)
-        load_weights(0)
-        load_table(gam[1], gamma, 1)
+        load_table(gam[0], gamma, 0)
         for j in range(PACK):
             load_plane(1, j)
+        load_weights(0)
+        load_table(gam[1], gamma, 1)
         load_weights(1)
-        load_table(gam[0], gamma, 0)
         load_table(bet[0], beta, 0)
         load_table(bet[1], beta, 1)
 
         for j in range(PACK):
             pick(0, j, 0, S)
-        look_up(g[1], gam[1])
+        look_up(g[0], gam[0])
         quantise(0, 0, S)
         multiply(0)
         for j in range(PACK - 1):
@@ -109,8 +109,8 @@ def tile_picked_cbn_none_e_kernel(tc, xT, w1_words, w1_scales, gamma, beta, offs
         quantise(1, 0, HALF)
         quantise(1, HALF, S)
         multiply(1)
-        look_up(g[0], gam[0])
-        scaled = [keep.tile([P, S], F32, name="scaled0"), keep.tile([P, S], F32, name="scaled1", tag="gam0")]
+        look_up(g[1], gam[1])
+        result = [keep.tile([P, S], F32, name="result0", tag="codes1", align_bytes=64), keep.tile([P, S], F32, name="result1")]
         for b in range(BLOCKS):
             nc.vector.tensor_tensor(scaled[b][:], acc[b][:], g[b][:], MULT)
         for b, lo, hi, queue in ((0, 0, S, nc.sync), (1, 0, HALF, nc.scalar), (1, HALF, S, nc.sync)):

@@ -32,14 +32,16 @@ def tile_picked_cbn_none_e_kernel(tc, xT, w1_words, w1_scales, gamma, beta, offs
         planes = [[keep.tile([P, T], F32, name=f"plane{z}{j}") for j in range(PACK)] for z in range(PASSES)]
         gam = [keep.tile([P, U], F32, name=f"gam{b}") for b in range(BLOCKS)]
         bet = [keep.tile([P, U], F32, name=f"bet{b}") for b in range(BLOCKS)]
-        w_words = [keep.tile([P, N], U32, name=f"w_words{z}", align_bytes=64) for z in range(PASSES)]
+        w_words = keep.tile([P, PASSES, N], U32, name="w_words", align_bytes=64)
         w_scales = keep.tile([P, PASSES, N], U8, name="w_scales", align_bytes=64)
         picked = [keep.tile([P, S, PACK], BF16, name=f"picked{z}", align_bytes=64) for z in range(PASSES)]
         codes = [keep.tile([P, S], U32, name=f"codes{z}", tag=f"codes{z}", align_bytes=64) for z in range(PASSES)]
         scales = [keep.tile([P, S], U8, name=f"scales{z}", align_bytes=64) for z in range(PASSES)]
-        g = [keep.tile([P, S], F32, name=f"g{b}") for b in range(BLOCKS)]
+        g0 = keep.tile([P, S], F32, name="g0")
+        y1 = keep.tile([P, S], F32, name="y1")
+        result = [keep.tile([P, S], F32, name=f"result{b}") for b in range(BLOCKS)]
         scaled = [keep.tile([P, S], F32, name=f"scaled{b}") for b in range(BLOCKS)]
-        acc = [psum.tile([P, S], F32, name=f"acc{b}") for b in range(BLOCKS)]
+        acc = [[psum.tile([P, HALF], F32, name=f"acc{b}{h}") for h in range(2)] for b in range(BLOCKS)]
 
         x_rows = xT.rearrange("(z p j) t -> z j p t", z=PASSES, j=PACK)
         scale_rows = w1_scales.rearrange("z (q r) c -> r q z c", r=4)
@@ -50,8 +52,8 @@ def tile_picked_cbn_none_e_kernel(tc, xT, w1_words, w1_scales, gamma, beta, offs
         def load_table(tile, table, b):
             nc.sync.dma_start(out=tile[:], in_=table[b * P : (b + 1) * P, :])
 
-        def load_weights(z):
-            nc.sync.dma_start(out=w_words[z][:].bitcast(I32), in_=w1_words[z].rearrange("p c r -> p (c r)").bitcast(I32))
+        def load_weights():
+            nc.sync.dma_start(out=w_words[:].bitcast(I32), in_=w1_words.rearrange("z p c r -> p z (c r)").bitcast(I32))
 
         def pick(z, j, lo, hi):
             nc.vector.tensor_copy(picked[z][:, lo:hi, j], planes[z][j][:].indirect(offs_t[:, lo // 16 : hi // 16]))
@@ -63,18 +65,16 @@ def tile_picked_cbn_none_e_kernel(tc, xT, w1_words, w1_scales, gamma, beta, offs
                 in_=picked[z][:, lo:hi, :].rearrange("p s j -> p (s j)"),
             )
 
-        def look_up(dst, tile):
-            nc.vector.tensor_copy(dst[:], tile[:].indirect(cls_t[:]))
-
-        def multiply(z):
-            for b in range(BLOCKS):
+        def multiply(z, h):
+            toks = slice(h * HALF, (h + 1) * HALF)
+            for b in (1, 0):
                 cols = slice(b * P, (b + 1) * P)
                 nc.tensor.matmul_mx(
-                    out=acc[b][:],
-                    lhsT=w_words[z][:, cols].bitcast(FP8X4),
+                    out=acc[b][h][:],
+                    lhsT=w_words[:, z, cols].bitcast(FP8X4),
                     lhsT_scale=w_scales[:, z, cols],
-                    rhs=codes[z][:].bitcast(FP8X4),
-                    rhs_scale=scales[z][:],
+                    rhs=codes[z][:, toks].bitcast(FP8X4),
+                    rhs_scale=scales[z][:, toks],
                     start=(z == 0),
                     stop=(z == PASSES - 1),
                 )
@@ -88,31 +88,33 @@ def tile_picked_cbn_none_e_kernel(tc, xT, w1_words, w1_scales, gamma, beta, offs
             nc.gpsimd.dma_start(out=w_scales[r:P:32, :, :].bitcast(I32), in_=scale_rows[r].bitcast(I32))
         load_plane(0, 2)
         load_plane(0, 3)
-        load_table(gam[0], gamma, 0)
         for j in range(PACK):
             load_plane(1, j)
-        load_weights(0)
+        load_weights()
+        load_table(gam[0], gamma, 0)
         load_table(gam[1], gamma, 1)
-        load_weights(1)
         load_table(bet[0], beta, 0)
         load_table(bet[1], beta, 1)
 
         for j in range(PACK):
             pick(0, j, 0, S)
-        look_up(g[0], gam[0])
         quantise(0, 0, S)
-        multiply(0)
+        multiply(0, 0)
+        multiply(0, 1)
         for j in range(PACK - 1):
             pick(1, j, 0, S)
         pick(1, PACK - 1, 0, HALF)
         pick(1, PACK - 1, HALF, S)
-        quantise(1, 0, HALF)
-        quantise(1, HALF, S)
-        multiply(1)
-        look_up(g[1], gam[1])
-        result = [keep.tile([P, S], F32, name="result0", tag="codes1", align_bytes=64), keep.tile([P, S], F32, name="result1")]
-        for b in range(BLOCKS):
-            nc.vector.tensor_tensor(scaled[b][:], acc[b][:], g[b][:], MULT)
+        for h in range(2):
+            quantise(1, h * HALF, (h + 1) * HALF)
+            multiply(1, h)
+            nc.scalar.copy(y1[:, h * HALF : (h + 1) * HALF], acc[1][h][:])
+        for lo, hi in ((0, HALF), (HALF, S)):
+            nc.vector.tensor_copy(g0[:, lo:hi], gam[0][:].indirect(cls_t[:, lo // 16 : hi // 16]))
+        for h in range(2):
+            toks = slice(h * HALF, (h + 1) * HALF)
+            nc.vector.tensor_tensor(scaled[0][:, toks], acc[0][h][:], g0[:, toks], MULT)
+        nc.vector.tensor_tensor(scaled[1][:], gam[1][:].indirect(cls_t[:]), y1[:], MULT)
         for b, lo, hi, queue in ((0, 0, S, nc.sync), (1, 0, HALF, nc.scalar), (1, HALF, S, nc.sync)):
             shift = bet[b][:].indirect(cls_t[:, lo // 16 : hi // 16])
             nc.vector.tensor_tensor(result[b][:, lo:hi], shift, scaled[b][:, lo:hi], ADD)

@@ -29,11 +29,13 @@ def tile_picked_cbn_none_e_kernel(tc, xT, w1_words, w1_scales, gamma, beta, offs
 
         offs_t = keep.tile([P, S // 16], U16, name="offs_t")
         cls_t = keep.tile([P, S // 16], U16, name="cls_t")
-        planes = [[keep.tile([P, T], F32, name=f"plane{z}{j}") for j in range(PACK)] for z in range(PASSES)]
+        pairs = [keep.tile([P, 2, T], F32, name=f"pair{i}") for i in range(3)]
+        dense = keep.tile([P, 2, S], F32, name="dense")
+        planes = {j: keep.tile([P, T], F32, name=f"plane{j}") for j in (2, 3)}
         gam = [keep.tile([P, U], F32, name=f"gam{b}") for b in range(BLOCKS)]
         bet = [keep.tile([P, U], F32, name=f"bet{b}") for b in range(BLOCKS)]
         w_words = keep.tile([P, PASSES, N], U32, name="w_words", align_bytes=64)
-        w_scales = keep.tile([P, PASSES, N], U8, name="w_scales", align_bytes=64)
+        w_scales = keep.tile([P, N], U8, name="w_scales", align_bytes=64)
         picked = [keep.tile([P, S, PACK], BF16, name=f"picked{z}", align_bytes=64) for z in range(PASSES)]
         codes = [keep.tile([P, S], U32, name=f"codes{z}", tag=f"codes{z}", align_bytes=64) for z in range(PASSES)]
         scales = [keep.tile([P, S], U8, name=f"scales{z}", align_bytes=64) for z in range(PASSES)]
@@ -44,10 +46,15 @@ def tile_picked_cbn_none_e_kernel(tc, xT, w1_words, w1_scales, gamma, beta, offs
         acc = [[psum.tile([P, HALF], F32, name=f"acc{b}{h}") for h in range(2)] for b in range(BLOCKS)]
 
         x_rows = xT.rearrange("(z p j) t -> z j p t", z=PASSES, j=PACK)
-        scale_rows = w1_scales.rearrange("z (q r) c -> r q z c", r=4)
+        x_pairs = xT.rearrange("(z p u e) t -> z u p e t", z=PASSES, u=2, e=2)
+        scale_rows = w1_scales.rearrange("z (q r) c -> q z r c", r=4)
 
-        def load_plane(z, j):
-            nc.sync.dma_start(out=planes[z][j][:], in_=x_rows[z, j])
+        def load_plane(j):
+            nc.sync.dma_start(out=planes[j][:], in_=x_rows[1, j])
+
+        def load_pair(i):
+            nc.sync.dma_start(out=pairs[i][:], in_=x_pairs[i // 2, i % 2])
+
 
         def load_table(tile, table, b):
             nc.sync.dma_start(out=tile[:], in_=table[b * P : (b + 1) * P, :])
@@ -55,8 +62,8 @@ def tile_picked_cbn_none_e_kernel(tc, xT, w1_words, w1_scales, gamma, beta, offs
         def load_weights():
             nc.sync.dma_start(out=w_words[:].bitcast(I32), in_=w1_words.rearrange("z p c r -> p z (c r)").bitcast(I32))
 
-        def pick(z, j, lo, hi):
-            nc.vector.tensor_copy(picked[z][:, lo:hi, j], planes[z][j][:].indirect(offs_t[:, lo // 16 : hi // 16]))
+        def pick(j, lo, hi):
+            nc.vector.tensor_copy(picked[1][:, lo:hi, j], planes[j][:].indirect(offs_t[:, lo // 16 : hi // 16]))
 
         def quantise(z, lo, hi):
             nc.vector.quantize_mx(
@@ -72,7 +79,7 @@ def tile_picked_cbn_none_e_kernel(tc, xT, w1_words, w1_scales, gamma, beta, offs
                 nc.tensor.matmul_mx(
                     out=acc[b][h][:],
                     lhsT=w_words[:, z, cols].bitcast(FP8X4),
-                    lhsT_scale=w_scales[:, z, cols],
+                    lhsT_scale=w_scales[4 * z : P, cols],
                     rhs=codes[z][:, toks].bitcast(FP8X4),
                     rhs_scale=scales[z][:, toks],
                     start=(z == 0),
@@ -80,31 +87,32 @@ def tile_picked_cbn_none_e_kernel(tc, xT, w1_words, w1_scales, gamma, beta, offs
                 )
 
         nc.gpsimd.memset(w_scales[:].bitcast(I32), 0)
-        load_plane(0, 0)
+        load_pair(0)
         nc.sync.dma_start(offs_t[:], offs)
-        load_plane(0, 1)
-        nc.sync.dma_start(cls_t[:], cls)
-        for r in range(4):
-            nc.gpsimd.dma_start(out=w_scales[r:P:32, :, :].bitcast(I32), in_=scale_rows[r].bitcast(I32))
-        load_plane(0, 2)
-        load_plane(0, 3)
-        for j in range(PACK):
-            load_plane(1, j)
+        load_pair(1)
+        load_pair(2)
+        load_plane(2)
+        load_plane(3)
+        for q in range(4):
+            nc.sync.dma_start(out=w_scales[32 * q : 32 * q + 8, :].bitcast(I32), in_=scale_rows[q].bitcast(I32))
         load_weights()
+        nc.sync.dma_start(cls_t[:], cls)
         load_table(gam[0], gamma, 0)
         load_table(gam[1], gamma, 1)
         load_table(bet[0], beta, 0)
         load_table(bet[1], beta, 1)
 
         for j in range(PACK):
-            pick(0, j, 0, S)
+            nc.vector.tensor_copy(picked[0][:, :, j], pairs[j // 2][:, j % 2, :].indirect(offs_t[:]))
         quantise(0, 0, S)
         multiply(0, 0)
         multiply(0, 1)
-        for j in range(PACK - 1):
-            pick(1, j, 0, S)
-        pick(1, PACK - 1, 0, HALF)
-        pick(1, PACK - 1, HALF, S)
+        for e in range(2):
+            nc.vector.tensor_copy(dense[:, e, :], pairs[2][:, e, :].indirect(offs_t[:]))
+        nc.scalar.copy(picked[1][:, :, 0:2], dense[:].rearrange("p e s -> p s e"))
+        pick(2, 0, S)
+        pick(3, 0, HALF)
+        pick(3, HALF, S)
         for h in range(2):
             quantise(1, h * HALF, (h + 1) * HALF)
             multiply(1, h)

@@ -39,11 +39,12 @@ def tile_picked_cbn_none_e_kernel(tc, xT, w1_words, w1_scales, gamma, beta, offs
         picked = [keep.tile([P, S, PACK], BF16, name=f"picked{z}", align_bytes=64) for z in range(PASSES)]
         codes = [keep.tile([P, S], U32, name=f"codes{z}", tag=f"codes{z}", align_bytes=64) for z in range(PASSES)]
         scales = [keep.tile([P, S], U8, name=f"scales{z}", align_bytes=64) for z in range(PASSES)]
-        g0 = keep.tile([P, S], F32, name="g0")
-        y1 = keep.tile([P, S], F32, name="y1")
+        g0 = keep.tile([P, HALF], F32, name="g0")
+        y = [keep.tile([P, S], F32, name=f"y{b}") for b in range(BLOCKS)]
         result = [keep.tile([P, S], F32, name=f"result{b}") for b in range(BLOCKS)]
         scaled = [keep.tile([P, S], F32, name=f"scaled{b}") for b in range(BLOCKS)]
-        acc = [[psum.tile([P, HALF], F32, name=f"acc{b}{h}") for h in range(2)] for b in range(BLOCKS)]
+        groups = [(0, 0, P), (0, P, HALF), (1, 0, HALF), (0, HALF, S), (1, HALF, S)]
+        acc = {(b, lo): psum.tile([P, hi - lo], F32, name=f"acc{b}_{lo}") for b, lo, hi in groups}
 
         x_rows = xT.rearrange("(z p j) t -> z j p t", z=PASSES, j=PACK)
         x_pairs = xT.rearrange("(z p u e) t -> z u p e t", z=PASSES, u=2, e=2)
@@ -72,21 +73,23 @@ def tile_picked_cbn_none_e_kernel(tc, xT, w1_words, w1_scales, gamma, beta, offs
                 in_=picked[z][:, lo:hi, :].rearrange("p s j -> p (s j)"),
             )
 
-        def multiply(z, h):
-            toks = slice(h * HALF, (h + 1) * HALF)
-            for b in (1, 0):
-                cols = slice(b * P, (b + 1) * P)
-                nc.tensor.matmul_mx(
-                    out=acc[b][h][:],
-                    lhsT=w_words[:, z, cols].bitcast(FP8X4),
-                    lhsT_scale=w_scales[4 * z : P, cols],
-                    rhs=codes[z][:, toks].bitcast(FP8X4),
-                    rhs_scale=scales[z][:, toks],
-                    start=(z == 0),
-                    stop=(z == PASSES - 1),
-                )
+        def multiply(z, b, lo, hi, start):
+            cols = slice(b * P, (b + 1) * P)
+            nc.tensor.matmul_mx(
+                out=acc[b, lo][:],
+                lhsT=w_words[:, z, cols].bitcast(FP8X4),
+                lhsT_scale=w_scales[4 * z : P, cols],
+                rhs=codes[z][:, lo:hi].bitcast(FP8X4),
+                rhs_scale=scales[z][:, lo:hi],
+                start=start,
+                stop=not start,
+            )
 
-        nc.gpsimd.memset(w_scales[:].bitcast(I32), 0)
+        def scale_fused(b, lo, hi):
+            factor = gam[b][:].indirect(cls_t[:, lo // 16 : hi // 16])
+            nc.vector.tensor_tensor(scaled[b][:, lo:hi], factor, y[b][:, lo:hi], MULT)
+
+        nc.vector.memset(w_scales[:].bitcast(I32), 0)
         load_pair(0)
         nc.sync.dma_start(offs_t[:], offs)
         load_pair(1)
@@ -105,25 +108,30 @@ def tile_picked_cbn_none_e_kernel(tc, xT, w1_words, w1_scales, gamma, beta, offs
         for j in range(PACK):
             nc.vector.tensor_copy(picked[0][:, :, j], pairs[j // 2][:, j % 2, :].indirect(offs_t[:]))
         quantise(0, 0, S)
-        multiply(0, 0)
-        multiply(0, 1)
+        for b, lo, hi in groups:
+            if lo < HALF:
+                multiply(0, b, lo, hi, True)
         for e in range(2):
             nc.vector.tensor_copy(dense[:, e, :], pairs[2][:, e, :].indirect(offs_t[:]))
         nc.scalar.copy(picked[1][:, :, 0:2], dense[:].rearrange("p e s -> p s e"))
         pick(2, 0, S)
         pick(3, 0, HALF)
         pick(3, HALF, S)
-        for h in range(2):
-            quantise(1, h * HALF, (h + 1) * HALF)
-            multiply(1, h)
-            nc.scalar.copy(y1[:, h * HALF : (h + 1) * HALF], acc[1][h][:])
-        for lo, hi in ((0, HALF), (HALF, S)):
-            nc.vector.tensor_copy(g0[:, lo:hi], gam[0][:].indirect(cls_t[:, lo // 16 : hi // 16]))
-        for h in range(2):
-            toks = slice(h * HALF, (h + 1) * HALF)
-            nc.vector.tensor_tensor(scaled[0][:, toks], acc[0][h][:], g0[:, toks], MULT)
-        nc.vector.tensor_tensor(scaled[1][:], gam[1][:].indirect(cls_t[:]), y1[:], MULT)
-        for b, lo, hi, queue in ((0, 0, S, nc.sync), (1, 0, HALF, nc.scalar), (1, HALF, S, nc.sync)):
+        for lo, hi in ((0, P), (P, HALF), (HALF, S)):
+            quantise(1, lo, hi)
+        for b, lo, hi in groups:
+            multiply(1, b, lo, hi, lo >= HALF)
+            if lo >= HALF:
+                multiply(0, b, lo, hi, False)
+            if (b, lo) != (0, HALF):
+                nc.scalar.copy(y[b][:, lo:hi], acc[b, lo][:])
+        nc.vector.tensor_copy(g0[:], gam[0][:].indirect(cls_t[:, HALF // 16 :]))
+        scale_fused(0, 0, P)
+        scale_fused(0, P, HALF)
+        nc.vector.tensor_tensor(scaled[0][:, HALF:], acc[0, HALF][:], g0[:], MULT)
+        scale_fused(1, 0, HALF)
+        scale_fused(1, HALF, S)
+        for b, lo, hi, queue in ((0, 0, S, nc.scalar), (1, 0, HALF, nc.sync), (1, HALF, S - P, nc.scalar), (1, S - P, S, nc.sync)):
             shift = bet[b][:].indirect(cls_t[:, lo // 16 : hi // 16])
             nc.vector.tensor_tensor(result[b][:, lo:hi], shift, scaled[b][:, lo:hi], ADD)
             queue.dma_start(out=out[b * P : (b + 1) * P, lo:hi], in_=result[b][:, lo:hi])

@@ -131,7 +131,7 @@ def tile_picked_cbn_none_e_kernel(tc, xT, w1_words, w1_scales, gamma, beta, offs
         nc.vector.tensor_tensor(scaled[0][:, HALF:], acc[0, HALF][:], g0[:], MULT)
         scale_fused(1, 0, HALF)
         scale_fused(1, HALF, S)
-        for b, lo, hi, queue in ((0, 0, S, nc.scalar), (1, 0, HALF, nc.sync), (1, HALF, S - P, nc.scalar), (1, S - P, S, nc.sync)):
+        for b, lo, hi in ((0, 0, S), (1, 0, HALF), (1, HALF, S - P), (1, S - P, S)):
             shift = bet[b][:].indirect(cls_t[:, lo // 16 : hi // 16])
             nc.vector.tensor_tensor(result[b][:, lo:hi], shift, scaled[b][:, lo:hi], ADD)
-            queue.dma_start(out=out[b * P : (b + 1) * P, lo:hi], in_=result[b][:, lo:hi])
+            nc.sync.dma_start(out=out[b * P : (b + 1) * P, lo:hi], in_=result[b][:, lo:hi])

@@ -47,14 +47,14 @@ def tile_picked_cbn_none_e_kernel(tc, xT, w1_words, w1_scales, gamma, beta, offs
         acc = {(b, lo): psum.tile([P, hi - lo], F32, name=f"acc{b}_{lo}") for b, lo, hi in groups}
 
         x_rows = xT.rearrange("(z p j) t -> z j p t", z=PASSES, j=PACK)
-        x_pairs = xT.rearrange("(z p u e) t -> z u p e t", z=PASSES, u=2, e=2)
         scale_rows = w1_scales.rearrange("z (q r) c -> q z r c", r=4)
 
         def load_plane(j):
             nc.sync.dma_start(out=planes[j][:], in_=x_rows[1, j])
 
         def load_pair(i):
-            nc.sync.dma_start(out=pairs[i][:], in_=x_pairs[i // 2, i % 2])
+            for e, queue in enumerate((nc.sync, nc.scalar)):
+                queue.dma_start(out=pairs[i][:, e, :], in_=x_rows[i // 2, 2 * (i % 2) + e])
 
 
         def load_table(tile, table, b):

@@ -94,10 +94,10 @@ def tile_picked_cbn_none_e_kernel(tc, xT, w1_words, w1_scales, gamma, beta, offs
         nc.sync.dma_start(offs_t[:], offs)
         load_pair(1)
         load_pair(2)
+        for q in range(4):
+            nc.scalar.dma_start(out=w_scales[32 * q : 32 * q + 8, :].bitcast(I32), in_=scale_rows[q].bitcast(I32))
         load_plane(2)
         load_plane(3)
-        for q in range(4):
-            nc.sync.dma_start(out=w_scales[32 * q : 32 * q + 8, :].bitcast(I32), in_=scale_rows[q].bitcast(I32))
         load_weights()
         nc.sync.dma_start(cls_t[:], cls)
         load_table(gam[0], gamma, 0)
@@ -109,8 +109,7 @@ def tile_picked_cbn_none_e_kernel(tc, xT, w1_words, w1_scales, gamma, beta, offs
             nc.vector.tensor_copy(picked[0][:, :, j], pairs[j // 2][:, j % 2, :].indirect(offs_t[:]))
         quantise(0, 0, S)
         for b, lo, hi in groups:
-            if lo < HALF:
-                multiply(0, b, lo, hi, True)
+            multiply(0, b, lo, hi, True)
         for e in range(2):
             nc.vector.tensor_copy(dense[:, e, :], pairs[2][:, e, :].indirect(offs_t[:]))
         nc.scalar.copy(picked[1][:, :, 0:2], dense[:].rearrange("p e s -> p s e"))
@@ -120,9 +119,7 @@ def tile_picked_cbn_none_e_kernel(tc, xT, w1_words, w1_scales, gamma, beta, offs
         for lo, hi in ((0, P), (P, HALF), (HALF, S)):
             quantise(1, lo, hi)
         for b, lo, hi in groups:
-            multiply(1, b, lo, hi, lo >= HALF)
-            if lo >= HALF:
-                multiply(0, b, lo, hi, False)
+            multiply(1, b, lo, hi, False)
             if (b, lo) != (0, HALF):
                 nc.scalar.copy(y[b][:, lo:hi], acc[b, lo][:])
         nc.vector.tensor_copy(g0[:], gam[0][:].indirect(cls_t[:, HALF // 16 :]))

@@ -18,6 +18,7 @@ PACK = 4
 PASSES = K // (P * PACK)
 BLOCKS = N // P
 HALF = S // 2
+HEAD = P + 32
 FLOPS = 2 * K * N * S
 
 
@@ -39,6 +40,7 @@ def tile_picked_cbn_none_e_kernel(tc, xT, w1_words, w1_scales, gamma, beta, offs
         picked = [keep.tile([P, S, PACK], BF16, name=f"picked{z}", align_bytes=64) for z in range(PASSES)]
         codes = [keep.tile([P, S], U32, name=f"codes{z}", tag=f"codes{z}", align_bytes=64) for z in range(PASSES)]
         scales = [keep.tile([P, S], U8, name=f"scales{z}", align_bytes=64) for z in range(PASSES)]
+        ends = {(lo, hi): keep.tile([P, hi - lo], BF16, name=f"end{lo}") for lo, hi in ((0, HEAD), (HEAD + HALF, S))}
         g0 = keep.tile([P, HALF], F32, name="g0")
         y = [keep.tile([P, S], F32, name=f"y{b}") for b in range(BLOCKS)]
         result = [keep.tile([P, S], F32, name=f"result{b}") for b in range(BLOCKS)]
@@ -114,8 +116,10 @@ def tile_picked_cbn_none_e_kernel(tc, xT, w1_words, w1_scales, gamma, beta, offs
             nc.vector.tensor_copy(dense[:, e, :], pairs[2][:, e, :].indirect(offs_t[:]))
         nc.scalar.copy(picked[1][:, :, 0:2], dense[:].rearrange("p e s -> p s e"))
         pick(2, 0, S)
-        pick(3, 0, HALF)
-        pick(3, HALF, S)
+        for (lo, hi), end in ends.items():
+            nc.vector.tensor_copy(end[:], planes[3][:].indirect(offs_t[:, lo // 16 : hi // 16]))
+            nc.scalar.copy(picked[1][:, lo:hi, 3], end[:])
+        pick(3, HEAD, HEAD + HALF)
         for lo, hi in ((0, P), (P, HALF), (HALF, S)):
             quantise(1, lo, hi)
         for b, lo, hi in groups:

@@ -11,6 +11,7 @@ U8 = mybir.dt.uint8
 FP8X4 = mybir.dt.float8_e4m3fn_x4
 MULT = mybir.AluOpType.mult
 ADD = mybir.AluOpType.add
+COPY = mybir.ActivationFunctionType.Copy
 
 K, T, S, N, U = 1024, 2048, 512, 256, 1024
 P = 128
@@ -18,7 +19,7 @@ PACK = 4
 PASSES = K // (P * PACK)
 BLOCKS = N // P
 HALF = S // 2
-HEAD = P + 32
+CUTS = ((128, 320, S), (192, 384, S))
 FLOPS = 2 * K * N * S
 
 
@@ -40,12 +41,12 @@ def tile_picked_cbn_none_e_kernel(tc, xT, w1_words, w1_scales, gamma, beta, offs
         picked = [keep.tile([P, S, PACK], BF16, name=f"picked{z}", align_bytes=64) for z in range(PASSES)]
         codes = [keep.tile([P, S], U32, name=f"codes{z}", tag=f"codes{z}", align_bytes=64) for z in range(PASSES)]
         scales = [keep.tile([P, S], U8, name=f"scales{z}", align_bytes=64) for z in range(PASSES)]
-        ends = {(lo, hi): keep.tile([P, hi - lo], BF16, name=f"end{lo}") for lo, hi in ((0, HEAD), (HEAD + HALF, S))}
-        g0 = keep.tile([P, HALF], F32, name="g0")
-        y = [keep.tile([P, S], F32, name=f"y{b}") for b in range(BLOCKS)]
+        factor = [keep.tile([P, S], F32, name=f"factor{b}") for b in range(BLOCKS)]
+        shift = [keep.tile([P, S], F32, name=f"shift{b}") for b in range(BLOCKS)]
         result = [keep.tile([P, S], F32, name=f"result{b}") for b in range(BLOCKS)]
         scaled = [keep.tile([P, S], F32, name=f"scaled{b}") for b in range(BLOCKS)]
-        groups = [(0, 0, P), (0, P, HALF), (1, 0, HALF), (0, HALF, S), (1, HALF, S)]
+        halves = ((0, HALF), (HALF, S))
+        groups = [(b, lo, hi) for lo, hi in halves for b in range(BLOCKS)]
         acc = {(b, lo): psum.tile([P, hi - lo], F32, name=f"acc{b}_{lo}") for b, lo, hi in groups}
 
         x_rows = xT.rearrange("(z p j) t -> z j p t", z=PASSES, j=PACK)
@@ -87,9 +88,18 @@ def tile_picked_cbn_none_e_kernel(tc, xT, w1_words, w1_scales, gamma, beta, offs
                 stop=not start,
             )
 
-        def scale_fused(b, lo, hi):
-            factor = gam[b][:].indirect(cls_t[:, lo // 16 : hi // 16])
-            nc.vector.tensor_tensor(scaled[b][:, lo:hi], factor, y[b][:, lo:hi], MULT)
+        def look_up(tile, table, lo, hi):
+            nc.scalar.activation(tile[:, lo:hi], table[:].indirect(cls_t[:, lo // 16 : hi // 16]), COPY)
+
+        def shift_fused(b, lo, hi):
+            looked_up = bet[b][:].indirect(cls_t[:, lo // 16 : hi // 16])
+            nc.vector.tensor_tensor(result[b][:, lo:hi], looked_up, scaled[b][:, lo:hi], ADD)
+
+        def shift_plain(b, lo, hi):
+            nc.vector.tensor_tensor(result[b][:, lo:hi], shift[b][:, lo:hi], scaled[b][:, lo:hi], ADD)
+
+        def store(b, lo, hi):
+            nc.sync.dma_start(out=out[b * P : (b + 1) * P, lo:hi], in_=result[b][:, lo:hi])
 
         nc.vector.memset(w_scales[:].bitcast(I32), 0)
         load_pair(0)
@@ -116,23 +126,26 @@ def tile_picked_cbn_none_e_kernel(tc, xT, w1_words, w1_scales, gamma, beta, offs
             nc.vector.tensor_copy(dense[:, e, :], pairs[2][:, e, :].indirect(offs_t[:]))
         nc.scalar.copy(picked[1][:, :, 0:2], dense[:].rearrange("p e s -> p s e"))
         pick(2, 0, S)
-        for (lo, hi), end in ends.items():
-            nc.vector.tensor_copy(end[:], planes[3][:].indirect(offs_t[:, lo // 16 : hi // 16]))
-            nc.scalar.copy(picked[1][:, lo:hi, 3], end[:])
-        pick(3, HEAD, HEAD + HALF)
-        for lo, hi in ((0, P), (P, HALF), (HALF, S)):
+        for lo, hi in halves:
+            pick(3, lo, hi)
+        for lo, hi in halves:
             quantise(1, lo, hi)
         for b, lo, hi in groups:
             multiply(1, b, lo, hi, False)
-            if (b, lo) != (0, HALF):
-                nc.scalar.copy(y[b][:, lo:hi], acc[b, lo][:])
-        nc.vector.tensor_copy(g0[:], gam[0][:].indirect(cls_t[:, HALF // 16 :]))
-        scale_fused(0, 0, P)
-        scale_fused(0, P, HALF)
-        nc.vector.tensor_tensor(scaled[0][:, HALF:], acc[0, HALF][:], g0[:], MULT)
-        scale_fused(1, 0, HALF)
-        scale_fused(1, HALF, S)
-        for b, lo, hi in ((0, 0, S), (1, 0, HALF), (1, HALF, S - P), (1, S - P, S)):
-            shift = bet[b][:].indirect(cls_t[:, lo // 16 : hi // 16])
-            nc.vector.tensor_tensor(result[b][:, lo:hi], shift, scaled[b][:, lo:hi], ADD)
-            nc.sync.dma_start(out=out[b * P : (b + 1) * P, lo:hi], in_=result[b][:, lo:hi])
+        for b in range(BLOCKS):
+            for lo, hi in halves:
+                look_up(factor[b], gam[b], lo, hi)
+                nc.vector.tensor_tensor(scaled[b][:, lo:hi], acc[b, lo][:], factor[b][:, lo:hi], MULT)
+        for b, cuts in enumerate(CUTS):
+            pieces = list(zip(cuts, cuts[1:]))
+            for lo, hi in pieces:
+                look_up(shift[b], bet[b], lo, hi)
+            shift_fused(b, 0, cuts[0])
+            if b == BLOCKS - 1:
+                store(b, 0, cuts[0])
+            for lo, hi in pieces:
+                shift_plain(b, lo, hi)
+                if b == BLOCKS - 1:
+                    store(b, lo, hi)
+            if b < BLOCKS - 1:
+                store(b, 0, S)

@@ -19,7 +19,8 @@ PACK = 4
 PASSES = K // (P * PACK)
 BLOCKS = N // P
 HALF = S // 2
-CUTS = ((128, 320, S), (192, 384, S))
+OWN = 128
+CUTS = ((128, 384, S), (160, 384, S))
 FLOPS = 2 * K * N * S
 
 
@@ -46,7 +47,7 @@ def tile_picked_cbn_none_e_kernel(tc, xT, w1_words, w1_scales, gamma, beta, offs
         result = [keep.tile([P, S], F32, name=f"result{b}") for b in range(BLOCKS)]
         scaled = [keep.tile([P, S], F32, name=f"scaled{b}") for b in range(BLOCKS)]
         halves = ((0, HALF), (HALF, S))
-        groups = [(b, lo, hi) for lo, hi in halves for b in range(BLOCKS)]
+        groups = [(b, lo, hi) for b in range(BLOCKS) for lo, hi in halves]
         acc = {(b, lo): psum.tile([P, hi - lo], F32, name=f"acc{b}_{lo}") for b, lo, hi in groups}
 
         x_rows = xT.rearrange("(z p j) t -> z j p t", z=PASSES, j=PACK)
@@ -113,8 +114,8 @@ def tile_picked_cbn_none_e_kernel(tc, xT, w1_words, w1_scales, gamma, beta, offs
         load_weights()
         nc.sync.dma_start(cls_t[:], cls)
         load_table(gam[0], gamma, 0)
-        load_table(gam[1], gamma, 1)
         load_table(bet[0], beta, 0)
+        load_table(gam[1], gamma, 1)
         load_table(bet[1], beta, 1)
 
         for j in range(PACK):
@@ -132,11 +133,12 @@ def tile_picked_cbn_none_e_kernel(tc, xT, w1_words, w1_scales, gamma, beta, offs
             quantise(1, lo, hi)
         for b, lo, hi in groups:
             multiply(1, b, lo, hi, False)
-        for b in range(BLOCKS):
-            for lo, hi in halves:
-                look_up(factor[b], gam[b], lo, hi)
-                nc.vector.tensor_tensor(scaled[b][:, lo:hi], acc[b, lo][:], factor[b][:, lo:hi], MULT)
         for b, cuts in enumerate(CUTS):
+            look_up(factor[b], gam[b], 0, HALF)
+            look_up(factor[b], gam[b], HALF, S - OWN)
+            nc.vector.tensor_copy(factor[b][:, S - OWN :], gam[b][:].indirect(cls_t[:, (S - OWN) // 16 :]))
+            for lo, hi in halves:
+                nc.vector.tensor_tensor(scaled[b][:, lo:hi], acc[b, lo][:], factor[b][:, lo:hi], MULT)
             pieces = list(zip(cuts, cuts[1:]))
             for lo, hi in pieces:
                 look_up(shift[b], bet[b], lo, hi)

@@ -19,8 +19,12 @@ PACK = 4
 PASSES = K // (P * PACK)
 BLOCKS = N // P
 HALF = S // 2
-OWN = 128
-CUTS = ((128, 384, S), (160, 384, S))
+SHARE = 192
+GROUPS = ((0, HALF, S), (0, HALF, S))
+OWN = ((384, S), (384, S))
+GAMMA_CUTS = (((0, HALF), (HALF, 384)), ((0, HALF), (HALF, 384)))
+PRODUCT_CUTS = ((0, HALF, S), (0, HALF, S))
+BETA_CUTS = ((128, 384, S), (160, 384, S))
 FLOPS = 2 * K * N * S
 
 
@@ -34,6 +38,7 @@ def tile_picked_cbn_none_e_kernel(tc, xT, w1_words, w1_scales, gamma, beta, offs
         cls_t = keep.tile([P, S // 16], U16, name="cls_t")
         pairs = [keep.tile([P, 2, T], F32, name=f"pair{i}") for i in range(3)]
         dense = keep.tile([P, 2, S], F32, name="dense")
+        ends = keep.tile([P, 2, SHARE], F32, name="ends")
         planes = {j: keep.tile([P, T], F32, name=f"plane{j}") for j in (2, 3)}
         gam = [keep.tile([P, U], F32, name=f"gam{b}") for b in range(BLOCKS)]
         bet = [keep.tile([P, U], F32, name=f"bet{b}") for b in range(BLOCKS)]
@@ -47,7 +52,7 @@ def tile_picked_cbn_none_e_kernel(tc, xT, w1_words, w1_scales, gamma, beta, offs
         result = [keep.tile([P, S], F32, name=f"result{b}") for b in range(BLOCKS)]
         scaled = [keep.tile([P, S], F32, name=f"scaled{b}") for b in range(BLOCKS)]
         halves = ((0, HALF), (HALF, S))
-        groups = [(b, lo, hi) for b in range(BLOCKS) for lo, hi in halves]
+        groups = [(b, lo, hi) for b in range(BLOCKS) for lo, hi in zip(GROUPS[b], GROUPS[b][1:])]
         acc = {(b, lo): psum.tile([P, hi - lo], F32, name=f"acc{b}_{lo}") for b, lo, hi in groups}
 
         x_rows = xT.rearrange("(z p j) t -> z j p t", z=PASSES, j=PACK)
@@ -123,22 +128,25 @@ def tile_picked_cbn_none_e_kernel(tc, xT, w1_words, w1_scales, gamma, beta, offs
         quantise(0, 0, S)
         for b, lo, hi in groups:
             multiply(0, b, lo, hi, True)
-        for e in range(2):
-            nc.vector.tensor_copy(dense[:, e, :], pairs[2][:, e, :].indirect(offs_t[:]))
+        nc.vector.tensor_copy(dense[:, 0, :], pairs[2][:, 0, :].indirect(offs_t[:]))
+        nc.scalar.activation(dense[:, 1, :], pairs[2][:, 1, :].indirect(offs_t[:]), COPY)
         nc.scalar.copy(picked[1][:, :, 0:2], dense[:].rearrange("p e s -> p s e"))
-        pick(2, 0, S)
-        for lo, hi in halves:
-            pick(3, lo, hi)
+        for e in range(2):
+            pick(2 + e, 0, S - SHARE)
+            nc.scalar.activation(ends[:, e, :], planes[2 + e][:].indirect(offs_t[:, (S - SHARE) // 16 :]), COPY)
+        nc.scalar.copy(picked[1][:, S - SHARE :, 2:4], ends[:].rearrange("p e s -> p s e"))
         for lo, hi in halves:
             quantise(1, lo, hi)
         for b, lo, hi in groups:
             multiply(1, b, lo, hi, False)
-        for b, cuts in enumerate(CUTS):
-            look_up(factor[b], gam[b], 0, HALF)
-            look_up(factor[b], gam[b], HALF, S - OWN)
-            nc.vector.tensor_copy(factor[b][:, S - OWN :], gam[b][:].indirect(cls_t[:, (S - OWN) // 16 :]))
-            for lo, hi in halves:
-                nc.vector.tensor_tensor(scaled[b][:, lo:hi], acc[b, lo][:], factor[b][:, lo:hi], MULT)
+        for b, cuts in enumerate(BETA_CUTS):
+            lo, hi = OWN[b]
+            nc.vector.tensor_copy(factor[b][:, lo:hi], gam[b][:].indirect(cls_t[:, lo // 16 : hi // 16]))
+            for lo, hi in GAMMA_CUTS[b]:
+                look_up(factor[b], gam[b], lo, hi)
+            for lo, hi in zip(PRODUCT_CUTS[b], PRODUCT_CUTS[b][1:]):
+                first = max(start for start in GROUPS[b] if start <= lo)
+                nc.vector.tensor_tensor(scaled[b][:, lo:hi], acc[b, first][:, lo - first : hi - first], factor[b][:, lo:hi], MULT)
             pieces = list(zip(cuts, cuts[1:]))
             for lo, hi in pieces:
                 look_up(shift[b], bet[b], lo, hi)

@@ -21,10 +21,10 @@ BLOCKS = N // P
 HALF = S // 2
 SHARE = 192
 GROUPS = ((0, HALF, S), (0, HALF, S))
-OWN = ((384, S), (384, S))
-GAMMA_CUTS = (((0, HALF), (HALF, 384)), ((0, HALF), (HALF, 384)))
+OWN = (((128, HALF), (384, S)), ((384, S),))
+GAMMA_CUTS = (((0, 128), (HALF, 384)), ((0, HALF), (HALF, 384)))
 PRODUCT_CUTS = ((0, HALF, S), (0, HALF, S))
-BETA_CUTS = ((128, 384, S), (160, 384, S))
+BETA_CUTS = ((128, 384, S), (192, 384, S))
 FLOPS = 2 * K * N * S
 
 
@@ -53,7 +53,8 @@ def tile_picked_cbn_none_e_kernel(tc, xT, w1_words, w1_scales, gamma, beta, offs
         scaled = [keep.tile([P, S], F32, name=f"scaled{b}") for b in range(BLOCKS)]
         halves = ((0, HALF), (HALF, S))
         groups = [(b, lo, hi) for b in range(BLOCKS) for lo, hi in zip(GROUPS[b], GROUPS[b][1:])]
-        acc = {(b, lo): psum.tile([P, hi - lo], F32, name=f"acc{b}_{lo}") for b, lo, hi in groups}
+        late = (1, 0, HALF)
+        acc = {(b, lo): psum.tile([P, hi - lo], F32, name=f"acc{b}_{lo}", tag=f"acc{b}_{lo}") for b, lo, hi in groups if (b, lo, hi) != late}
 
         x_rows = xT.rearrange("(z p j) t -> z j p t", z=PASSES, j=PACK)
         scale_rows = w1_scales.rearrange("z (q r) c -> q z r c", r=4)
@@ -127,7 +128,8 @@ def tile_picked_cbn_none_e_kernel(tc, xT, w1_words, w1_scales, gamma, beta, offs
             nc.vector.tensor_copy(picked[0][:, :, j], pairs[j // 2][:, j % 2, :].indirect(offs_t[:]))
         quantise(0, 0, S)
         for b, lo, hi in groups:
-            multiply(0, b, lo, hi, True)
+            if (b, lo, hi) != late:
+                multiply(0, b, lo, hi, True)
         nc.vector.tensor_copy(dense[:, 0, :], pairs[2][:, 0, :].indirect(offs_t[:]))
         nc.scalar.activation(dense[:, 1, :], pairs[2][:, 1, :].indirect(offs_t[:]), COPY)
         nc.scalar.copy(picked[1][:, :, 0:2], dense[:].rearrange("p e s -> p s e"))
@@ -138,10 +140,15 @@ def tile_picked_cbn_none_e_kernel(tc, xT, w1_words, w1_scales, gamma, beta, offs
         for lo, hi in halves:
             quantise(1, lo, hi)
         for b, lo, hi in groups:
-            multiply(1, b, lo, hi, False)
+            if (b, lo, hi) != late:
+                multiply(1, b, lo, hi, False)
         for b, cuts in enumerate(BETA_CUTS):
-            lo, hi = OWN[b]
-            nc.vector.tensor_copy(factor[b][:, lo:hi], gam[b][:].indirect(cls_t[:, lo // 16 : hi // 16]))
+            if b == late[0]:
+                acc[1, 0] = psum.tile([P, HALF], F32, name="acc1_0", tag="acc0_0")
+                for z in range(PASSES):
+                    multiply(z, *late, z == 0)
+            for lo, hi in OWN[b]:
+                nc.vector.tensor_copy(factor[b][:, lo:hi], gam[b][:].indirect(cls_t[:, lo // 16 : hi // 16]))
             for lo, hi in GAMMA_CUTS[b]:
                 look_up(factor[b], gam[b], lo, hi)
             for lo, hi in zip(PRODUCT_CUTS[b], PRODUCT_CUTS[b][1:]):

@@ -21,10 +21,10 @@ BLOCKS = N // P
 HALF = S // 2
 SHARE = 192
 GROUPS = ((0, HALF, S), (0, HALF, S))
-OWN = (((128, HALF), (384, S)), ((384, S),))
-GAMMA_CUTS = (((0, 128), (HALF, 384)), ((0, HALF), (HALF, 384)))
+OWN = (((128, HALF), (384, S)), ((160, HALF), (HALF, 384)))
+GAMMA_CUTS = (((0, 128), (HALF, 384)), ((0, 160), (384, S)))
 PRODUCT_CUTS = ((0, HALF, S), (0, HALF, S))
-BETA_CUTS = ((128, 384, S), (192, 384, S))
+BETA_CUTS = ((128, 384, S), (224, 384, S))
 FLOPS = 2 * K * N * S
 
 
@@ -103,7 +103,8 @@ def tile_picked_cbn_none_e_kernel(tc, xT, w1_words, w1_scales, gamma, beta, offs
             nc.vector.tensor_tensor(result[b][:, lo:hi], looked_up, scaled[b][:, lo:hi], ADD)
 
         def shift_plain(b, lo, hi):
-            nc.vector.tensor_tensor(result[b][:, lo:hi], shift[b][:, lo:hi], scaled[b][:, lo:hi], ADD)
+            engine = nc.gpsimd if b == 0 else nc.vector
+            engine.tensor_tensor(result[b][:, lo:hi], shift[b][:, lo:hi], scaled[b][:, lo:hi], ADD)
 
         def store(b, lo, hi):
             nc.sync.dma_start(out=out[b * P : (b + 1) * P, lo:hi], in_=result[b][:, lo:hi])

@@ -21,8 +21,8 @@ BLOCKS = N // P
 HALF = S // 2
 SHARE = 192
 GROUPS = ((0, HALF, S), (0, HALF, S))
-OWN = (((128, HALF), (384, S)), ((160, HALF), (HALF, 384)))
-GAMMA_CUTS = (((0, 128), (HALF, 384)), ((0, 160), (384, S)))
+OWN = (((160, HALF), (416, S)), ((128, HALF), (HALF, 384)))
+GAMMA_CUTS = (((0, 160), (HALF, 416)), ((0, 128), (384, S)))
 PRODUCT_CUTS = ((0, HALF, S), (0, HALF, S))
 BETA_CUTS = ((128, 384, S), (224, 384, S))
 FLOPS = 2 * K * N * S

from contextlib import ExitStack

import concourse.mybir as mybir

F32 = mybir.dt.float32
BF16 = mybir.dt.bfloat16
I32 = mybir.dt.int32
U32 = mybir.dt.uint32
U16 = mybir.dt.uint16
U8 = mybir.dt.uint8
FP8X4 = mybir.dt.float8_e4m3fn_x4
MULT = mybir.AluOpType.mult
ADD = mybir.AluOpType.add
COPY = mybir.ActivationFunctionType.Copy

K, T, S, N, U = 1024, 2048, 512, 256, 1024
P = 128
PACK = 4
PASSES = K // (P * PACK)
BLOCKS = N // P
HALF = S // 2
SHARE = 192
GROUPS = ((0, HALF, S), (0, HALF, S))
OWN = (((160, HALF), (416, S)), ((128, HALF), (HALF, 384)))
GAMMA_CUTS = (((0, 160), (HALF, 416)), ((0, 128), (384, S)))
PRODUCT_CUTS = ((0, HALF, S), (0, HALF, S))
BETA_CUTS = ((128, 384, S), (224, 384, S))
FLOPS = 2 * K * N * S


def tile_picked_cbn_none_e_kernel(tc, xT, w1_words, w1_scales, gamma, beta, offs, cls, out):
    nc = tc.nc
    with ExitStack() as ctx:
        keep = ctx.enter_context(tc.tile_pool(name="keep", bufs=1))
        psum = ctx.enter_context(tc.psum_pool(name="psum", bufs=1))

        offs_t = keep.tile([P, S // 16], U16, name="offs_t")
        cls_t = keep.tile([P, S // 16], U16, name="cls_t")
        pairs = [keep.tile([P, 2, T], F32, name=f"pair{i}") for i in range(3)]
        dense = keep.tile([P, 2, S], F32, name="dense")
        ends = keep.tile([P, 2, SHARE], F32, name="ends")
        planes = {j: keep.tile([P, T], F32, name=f"plane{j}") for j in (2, 3)}
        gam = [keep.tile([P, U], F32, name=f"gam{b}") for b in range(BLOCKS)]
        bet = [keep.tile([P, U], F32, name=f"bet{b}") for b in range(BLOCKS)]
        w_words = keep.tile([P, PASSES, N], U32, name="w_words", align_bytes=64)
        w_scales = keep.tile([P, N], U8, name="w_scales", align_bytes=64)
        picked = [keep.tile([P, S, PACK], BF16, name=f"picked{z}", align_bytes=64) for z in range(PASSES)]
        codes = [keep.tile([P, S], U32, name=f"codes{z}", tag=f"codes{z}", align_bytes=64) for z in range(PASSES)]
        scales = [keep.tile([P, S], U8, name=f"scales{z}", align_bytes=64) for z in range(PASSES)]
        factor = [keep.tile([P, S], F32, name=f"factor{b}") for b in range(BLOCKS)]
        shift = [keep.tile([P, S], F32, name=f"shift{b}") for b in range(BLOCKS)]
        result = [keep.tile([P, S], F32, name=f"result{b}") for b in range(BLOCKS)]
        scaled = [keep.tile([P, S], F32, name=f"scaled{b}") for b in range(BLOCKS)]
        halves = ((0, HALF), (HALF, S))
        groups = [(b, lo, hi) for b in range(BLOCKS) for lo, hi in zip(GROUPS[b], GROUPS[b][1:])]
        late = (1, 0, HALF)
        acc = {(b, lo): psum.tile([P, hi - lo], F32, name=f"acc{b}_{lo}", tag=f"acc{b}_{lo}") for b, lo, hi in groups if (b, lo, hi) != late}

        x_rows = xT.rearrange("(z p j) t -> z j p t", z=PASSES, j=PACK)
        scale_rows = w1_scales.rearrange("z (q r) c -> q z r c", r=4)

        def load_plane(j):
            nc.sync.dma_start(out=planes[j][:], in_=x_rows[1, j])

        def load_pair(i):
            for e, queue in enumerate((nc.sync, nc.scalar)):
                queue.dma_start(out=pairs[i][:, e, :], in_=x_rows[i // 2, 2 * (i % 2) + e])


        def load_table(tile, table, b):
            nc.sync.dma_start(out=tile[:], in_=table[b * P : (b + 1) * P, :])

        def load_weights():
            nc.sync.dma_start(out=w_words[:].bitcast(I32), in_=w1_words.rearrange("z p c r -> p z (c r)").bitcast(I32))

        def pick(j, lo, hi):
            nc.vector.tensor_copy(picked[1][:, lo:hi, j], planes[j][:].indirect(offs_t[:, lo // 16 : hi // 16]))

        def quantise(z, lo, hi):
            nc.vector.quantize_mx(
                out=codes[z][:, lo:hi].bitcast(FP8X4),
                scales=scales[z][:, lo:hi],
                in_=picked[z][:, lo:hi, :].rearrange("p s j -> p (s j)"),
            )

        def multiply(z, b, lo, hi, start):
            cols = slice(b * P, (b + 1) * P)
            nc.tensor.matmul_mx(
                out=acc[b, lo][:],
                lhsT=w_words[:, z, cols].bitcast(FP8X4),
                lhsT_scale=w_scales[4 * z : P, cols],
                rhs=codes[z][:, lo:hi].bitcast(FP8X4),
                rhs_scale=scales[z][:, lo:hi],
                start=start,
                stop=not start,
            )

        def look_up(tile, table, lo, hi):
            nc.scalar.activation(tile[:, lo:hi], table[:].indirect(cls_t[:, lo // 16 : hi // 16]), COPY)

        def shift_fused(b, lo, hi):
            looked_up = bet[b][:].indirect(cls_t[:, lo // 16 : hi // 16])
            nc.vector.tensor_tensor(result[b][:, lo:hi], looked_up, scaled[b][:, lo:hi], ADD)

        def shift_plain(b, lo, hi):
            engine = nc.gpsimd if b == 0 else nc.vector
            engine.tensor_tensor(result[b][:, lo:hi], shift[b][:, lo:hi], scaled[b][:, lo:hi], ADD)

        def store(b, lo, hi):
            nc.sync.dma_start(out=out[b * P : (b + 1) * P, lo:hi], in_=result[b][:, lo:hi])

        nc.vector.memset(w_scales[:].bitcast(I32), 0)
        load_pair(0)
        nc.sync.dma_start(offs_t[:], offs)
        load_pair(1)
        load_pair(2)
        for q in range(4):
            nc.scalar.dma_start(out=w_scales[32 * q : 32 * q + 8, :].bitcast(I32), in_=scale_rows[q].bitcast(I32))
        load_plane(2)
        load_plane(3)
        load_weights()
        nc.sync.dma_start(cls_t[:], cls)
        load_table(gam[0], gamma, 0)
        load_table(bet[0], beta, 0)
        load_table(gam[1], gamma, 1)
        load_table(bet[1], beta, 1)

        for j in range(PACK):
            nc.vector.tensor_copy(picked[0][:, :, j], pairs[j // 2][:, j % 2, :].indirect(offs_t[:]))
        quantise(0, 0, S)
        for b, lo, hi in groups:
            if (b, lo, hi) != late:
                multiply(0, b, lo, hi, True)
        nc.vector.tensor_copy(dense[:, 0, :], pairs[2][:, 0, :].indirect(offs_t[:]))
        nc.scalar.activation(dense[:, 1, :], pairs[2][:, 1, :].indirect(offs_t[:]), COPY)
        nc.scalar.copy(picked[1][:, :, 0:2], dense[:].rearrange("p e s -> p s e"))
        for e in range(2):
            pick(2 + e, 0, S - SHARE)
            nc.scalar.activation(ends[:, e, :], planes[2 + e][:].indirect(offs_t[:, (S - SHARE) // 16 :]), COPY)
        nc.scalar.copy(picked[1][:, S - SHARE :, 2:4], ends[:].rearrange("p e s -> p s e"))
        for lo, hi in halves:
            quantise(1, lo, hi)
        for b, lo, hi in groups:
            if (b, lo, hi) != late:
                multiply(1, b, lo, hi, False)
        for b, cuts in enumerate(BETA_CUTS):
            if b == late[0]:
                acc[1, 0] = psum.tile([P, HALF], F32, name="acc1_0", tag="acc0_0")
                for z in range(PASSES):
                    multiply(z, *late, z == 0)
            for lo, hi in OWN[b]:
                nc.vector.tensor_copy(factor[b][:, lo:hi], gam[b][:].indirect(cls_t[:, lo // 16 : hi // 16]))
            for lo, hi in GAMMA_CUTS[b]:
                look_up(factor[b], gam[b], lo, hi)
            for lo, hi in zip(PRODUCT_CUTS[b], PRODUCT_CUTS[b][1:]):
                first = max(start for start in GROUPS[b] if start <= lo)
                nc.vector.tensor_tensor(scaled[b][:, lo:hi], acc[b, first][:, lo - first : hi - first], factor[b][:, lo:hi], MULT)
            pieces = list(zip(cuts, cuts[1:]))
            for lo, hi in pieces:
                look_up(shift[b], bet[b], lo, hi)
            shift_fused(b, 0, cuts[0])
            if b == BLOCKS - 1:
                store(b, 0, cuts[0])
            for lo, hi in pieces:
                shift_plain(b, lo, hi)
                if b == BLOCKS - 1:
                    store(b, lo, hi)
            if b < BLOCKS - 1:
                store(b, 0, S)
